import numpy as np
import ml_dtypes


def mxq(x, axis, fmt="e4m3"):
    dtype, down = {"e4m3": (ml_dtypes.float8_e4m3fn, 7), "e5m2": (ml_dtypes.float8_e5m2, 14)}[fmt]
    v = np.moveaxis(np.asarray(x, np.float32).astype(ml_dtypes.bfloat16).astype(np.float64), axis, -1)
    blocks = v.reshape(v.shape[:-1] + (-1, 32))
    amax = np.abs(blocks).max(-1, keepdims=True)
    byte = np.maximum(np.where(amax > 0, np.frexp(amax)[1] - 1 + 127, 0) - down, 1)
    scale = np.exp2(byte - 127.0)
    codes = (blocks / scale).astype(np.float32).astype(dtype).astype(np.float64)
    return np.moveaxis((codes * scale).reshape(v.shape), -1, axis)


WIDE = False


def mx_kscale(k):
    if not WIDE:
        return np.ones(k)
    levels = np.array([10, -10, 5, -5, 0])
    if k % 512:
        return np.exp2(np.random.permutation(np.resize(levels, k // 32))).repeat(32)
    a = np.empty((k // 512, 16))
    for p in range(k // 512):
        a[p, :8] = np.random.permutation(np.resize(levels, 8))
        for g in range(8):
            far = levels[np.abs(levels - a[p, g]) >= 10]
            a[p, g + 8] = far[np.random.randint(len(far))]
    return np.exp2(a.ravel()).repeat(32)


def f64(x):
    return np.asarray(x).astype(np.float64)


def striped(idx):
    return np.tile(idx.reshape(-1, 16).T, (8, 1)).astype(np.uint16)


def unstriped(offs):
    return offs[:16].T.reshape(-1).astype(np.int64)


E2M1 = np.array([0.0, 0.5, 1.0, 1.5, 2.0, 3.0, 4.0, 6.0, -0.0, -0.5, -1.0, -1.5, -2.0, -3.0, -4.0, -6.0])


def pack_weight(w, fmt):
    k, n = w.shape
    w = f64(np.asarray(w, np.float32).astype(ml_dtypes.bfloat16)).reshape(k // 32, 32, n)
    amax = np.abs(w).max(1)
    if fmt == "e4m3":
        byte = np.frexp(amax)[1] - 1 + 127 - 7
    else:
        mant, ex = np.frexp(amax / 6.0)
        byte = np.where(mant > 0.5, ex, ex - 1) + 127
    byte = np.clip(np.where(amax > 0, byte, 1), 1, 254)
    scaled = (w * np.exp2(127.0 - byte)[:, None, :]).reshape(k, n).astype(np.float32)
    by_word = np.ascontiguousarray(scaled.reshape(k // 512, 128, 4, n).transpose(0, 1, 3, 2))
    if fmt == "e4m3":
        words = by_word.astype(ml_dtypes.float8_e4m3fn).view(np.uint8)
    else:
        c = by_word.astype(ml_dtypes.float4_e2m1fn).view(np.uint8) & 0xF
        words = (c[..., 0::2] | (c[..., 1::2] << 4)).reshape(k // 512, 128, 2 * n)
    return np.ascontiguousarray(words), np.ascontiguousarray(byte.astype(np.uint8).reshape(k // 512, 16, n))


def unpack_weight(words, scales, fmt):
    g, _, n = scales.shape
    words = np.ascontiguousarray(words).reshape(g, 128, n, -1)
    if fmt == "e4m3":
        vals = words.view(ml_dtypes.float8_e4m3fn).astype(np.float64)
    else:
        nib = np.empty((g, 128, n, 4), np.uint8)
        nib[..., 0::2] = words & 0xF
        nib[..., 1::2] = words >> 4
        vals = E2M1[nib]
    vals = vals * np.repeat(np.exp2(scales.astype(np.float64) - 127.0), 8, axis=1)[..., None]
    return vals.transpose(0, 1, 3, 2).reshape(g * 512, n)


def gelu(v):
    return 0.5 * v * (1.0 + np.tanh(np.sqrt(2.0 / np.pi) * (v + 0.044715 * v**3)))


K, H, T, S, T2, P = 1024, 512, 4096, 1024, 2048, 1024

def setup_inputs():
    n = np.random.standard_normal
    s = mx_kscale(K)[:, None]
    u = mx_kscale(H)[:, None]
    d = {}
    d["tab_words"], d["tab_scales"] = pack_weight(n((K, T)) * s, "e4m3")
    d["offs"] = striped(np.random.permutation(T)[:S])
    d["offs2"] = striped(np.random.permutation(T2)[:S])
    d["offs3"] = striped(np.random.permutation(T2)[:P])
    d["offs4"] = striped(np.random.permutation(T2)[:P])
    d["w1"] = (n((K, H)) / K ** 0.5 / s * u.T).astype(np.float32)
    d["w2_words"], d["w2_scales"] = pack_weight(n((K, H)) / K ** 0.5 / s * u.T, "e2m1")
    d["w3"] = (n((K, H)) / K ** 0.5 / s).astype(np.float32)
    d["wgs"] = np.exp(0.3 * n((128, S))).astype(np.float32)
    d["page0"] = (1.5 * n((H, T2)) * u).astype(np.float32)
    d["sc"] = np.exp(0.3 * n(H)).astype(np.float32)
    d["w4"] = (0.7 * n((H, H)) / H ** 0.5 / u).astype(np.float32)
    d["w5_words"], d["w5_scales"] = pack_weight(n((H, H)) / H ** 0.5 / u, "e4m3")
    d["gf"] = (0.7 * np.exp(0.3 * n(H)) / u[:, 0]).astype(np.float32)
    return d

def reference(tab_words, tab_scales, offs, offs2, offs3, offs4, w1, w2_words, w2_scales, w3,
              wgs, page0, sc, w4, w5_words, w5_scales, gf):
    v = unpack_weight(tab_words, tab_scales, "e4m3")[:, unstriped(offs)]
    a = mxq(f64(w1), 0, "e4m3").T @ v
    b = unpack_weight(w2_words, w2_scales, "e2m1").T @ v
    c = mxq(f64(w3), 0, "e4m3").T @ v
    h = np.abs(a - b) * c + b
    page = f64(page0).copy()
    page[:, unstriped(offs2)] = np.tile(f64(wgs), (H // 128, 1)) * h
    x = f64(sc)[:, None] * page[:, unstriped(offs3)]
    xq = mxq(x, 0, "e4m3")
    p = mxq(f64(w4), 0, "e4m3").T @ xq
    q = unpack_weight(w5_words, w5_scales, "e4m3").T @ xq
    y = q * np.tanh(p)
    return y + f64(gf)[:, None] * page[:, unstriped(offs4)]

@@ -1,0 +1,358 @@
+from contextlib import ExitStack
+
+import concourse.mybir as mybir
+from concourse.masks import make_identity
+
+K, H, T, S, T2, M = 1024, 512, 4096, 1024, 2048, 1024
+FLOPS = 2 * (3 * K * H * S + 2 * H * H * M)
+
+F32 = mybir.dt.float32
+BF16 = mybir.dt.bfloat16
+I32 = mybir.dt.int32
+U32 = mybir.dt.uint32
+U16 = mybir.dt.uint16
+U8 = mybir.dt.uint8
+FP8X4 = mybir.dt.float8_e4m3fn_x4
+FP4X4 = mybir.dt.float4_e2m1fn_x4
+ALU = mybir.AluOpType
+ACT = mybir.ActivationFunctionType
+
+P = 128
+PACK = 4
+PASSES = K // (P * PACK)
+TILES = H // P
+HALF = 512
+BLOCKS = HALF // P
+COLS = HALF // 16
+SUMMED_IN_PSUM = (2, 4, 6)
+
+
+def tile_list_lint_classing_step_kernel(
+    tc, tab_words, tab_scales, offs, offs2, offs3, offs4, w1, w2_words, w2_scales, w3,
+    wgs, page0, sc, w4, w5_words, w5_scales, gf, out,
+):
+    nc = tc.nc
+    with ExitStack() as ctx:
+        lists = ctx.enter_context(tc.tile_pool(name="lists", bufs=1))
+        keep = ctx.enter_context(tc.tile_pool(name="keep", bufs=1))
+        work = ctx.enter_context(tc.tile_pool(name="work", bufs=2))
+        psum = ctx.enter_context(tc.psum_pool(name="psum", bufs=2))
+
+        def load_list(src, name):
+            tile = lists.tile([P, S // 16], U16, name=name)
+            nc.sync.dma_start(tile[:], src)
+            return tile
+
+        def half_list(tile, hf):
+            return tile[:, hf * COLS:(hf + 1) * COLS]
+
+        tab_sc = keep.tile([P, T], U8, name="tab_sc", align_bytes=64)
+        nc.sync.dma_start(
+            out=tab_sc[0:32, :].bitcast(I32), in_=tab_scales.rearrange("a q n -> (a q) n").bitcast(I32)
+        )
+        nc.vector.memset(tab_sc[32:64, :].bitcast(I32), 0)
+        nc.vector.memset(tab_sc[64:P, :].bitcast(I32), 0)
+        w2_sc = keep.tile([P, PASSES * H], U8, name="w2_sc", align_bytes=64)
+        nc.gpsimd.memset(w2_sc[:].bitcast(I32), 0)
+        for q in range(4):
+            nc.scalar.dma_start(
+                out=w2_sc[32 * q:32 * q + 4, :].bitcast(I32).rearrange("r (a c) -> r a c", a=PASSES),
+                in_=w2_scales[:, 4 * q:4 * q + 4, :].bitcast(I32).rearrange("a r c -> r a c"),
+            )
+        v_planes = keep.tile([P, PASSES * S], U8, name="v_planes", align_bytes=64)
+        nc.vector.memset(v_planes[:].bitcast(I32), 0)
+        w5_sc = keep.tile([P, H], U8, name="w5_sc", align_bytes=64)
+        nc.vector.memset(w5_sc[:].bitcast(I32), 0)
+
+        warm_in = keep.tile([P, 1], F32, name="warm_in")
+        nc.vector.memset(warm_in[:], 0.0)
+        warm_out = keep.tile([P, 1], F32, name="warm_out")
+        nc.scalar.activation(warm_out[:], warm_in[:], ACT.Tanh)
+
+        ident32 = keep.tile([P, P], F32, name="ident32")
+        make_identity(nc, ident32[:])
+        ident16 = keep.tile([P, P], BF16, name="ident16")
+        make_identity(nc, ident16[:])
+
+        list1 = load_list(offs, "list1")
+        tab_w = []
+        for a in range(PASSES):
+            tile = keep.tile([P, T], U32, name="tab_w%d" % a)
+            nc.sync.dma_start(
+                out=tile[:].bitcast(I32), in_=tab_words[a].rearrange("p n i -> p (n i)").bitcast(I32)
+            )
+            tab_w.append(tile)
+        w2_w = keep.tile([P, PASSES * 2 * H], U8, name="w2_w", align_bytes=64)
+        nc.sync.dma_start(
+            out=w2_w[:].bitcast(I32).rearrange("p (a n) -> p a n", a=PASSES),
+            in_=w2_words.bitcast(I32).rearrange("a p n -> p a n"),
+        )
+
+        raw = {}
+
+        def load_weights(t):
+            for name, w in (("w1", w1), ("w3", w3)):
+                for a in range(PASSES):
+                    tile = keep.tile([P, PACK, P], F32, name="raw_%s_%d_%d" % (name, t, a))
+                    nc.sync.dma_start(
+                        out=tile[:],
+                        in_=w[a * 512:(a + 1) * 512, t * P:(t + 1) * P].rearrange("(p j) c -> p j c", j=PACK),
+                    )
+                    raw[(name, t, a)] = tile
+
+        page = []
+
+        def load_page(t):
+            tile = keep.tile([P, T2], F32, name="page%d" % t)
+            nc.sync.dma_start(out=tile[:], in_=page0[t * P:(t + 1) * P, :])
+            page.append(tile)
+
+        load_weights(0)
+        list2 = load_list(offs2, "list2")
+        wgs0 = keep.tile([P, HALF], F32, name="wgs0")
+        nc.sync.dma_start(out=wgs0[:], in_=wgs[:, 0:HALF])
+        load_page(0)
+        wgs1 = keep.tile([P, HALF], F32, name="wgs1", tag="after_scatter")
+        nc.sync.dma_start(out=wgs1[:], in_=wgs[:, HALF:S])
+        wgs_half = [wgs0, wgs1]
+        load_weights(1)
+        list3 = load_list(offs3, "list3")
+        sc_col = keep.tile([P, TILES], F32, name="sc_col")
+        gf_col = keep.tile([P, TILES], F32, name="gf_col")
+        with nc.allow_non_contiguous_dma(reason="one value for each row of a tile"):
+            nc.sync.dma_start(out=sc_col[:], in_=sc.rearrange("(t p) -> p t", p=P))
+        load_weights(2)
+        load_page(1)
+        load_weights(3)
+        load_page(2)
+        load_page(3)
+        raw_w4 = keep.tile([P, PACK, H], F32, name="raw_w4")
+        nc.sync.dma_start(out=raw_w4[:], in_=w4.rearrange("(p j) c -> p j c", j=PACK))
+        w5_w = keep.tile([P, H], U32, name="w5_w", align_bytes=64)
+        nc.sync.dma_start(
+            out=w5_w[:].bitcast(I32), in_=w5_words[0].rearrange("p n i -> p (n i)").bitcast(I32)
+        )
+        for q in range(4):
+            nc.sync.dma_start(
+                out=w5_sc[32 * q:32 * q + 4, :].bitcast(I32),
+                in_=w5_scales[0, 4 * q:4 * q + 4, :].bitcast(I32),
+            )
+        list4 = load_list(offs4, "list4")
+        with nc.allow_non_contiguous_dma(reason="one value for each row of a tile"):
+            nc.sync.dma_start(out=gf_col[:], in_=gf.rearrange("(t p) -> p t", p=P))
+
+        v_sc = keep.tile([P, S], U8, name="v_sc", align_bytes=64)
+        nc.vector.tensor_copy(v_sc[:], tab_sc[:].indirect(list1[:]))
+        for a in range(PASSES):
+            for q in range(4):
+                nc.scalar.dma_start(
+                    out=v_planes[32 * q:32 * q + 4, a * S:(a + 1) * S].bitcast(I32),
+                    in_=v_sc[16 * a + 4 * q:16 * a + 4 * q + 4, :].bitcast(I32),
+                )
+        v_w = {}
+        for a in range(PASSES):
+            for hf in range(2):
+                tile = keep.tile([P, HALF], U32, name="v_w%d_%d" % (a, hf), align_bytes=64)
+                nc.vector.tensor_copy(tile[:], tab_w[a][:].indirect(half_list(list1, hf)))
+                v_w[(a, hf)] = tile
+
+        def interleave(dst, src, sign=1.0, on_vector=False):
+            dst = dst.rearrange("p (c i j) -> p c j i", i=4, j=PACK)
+            src = src.rearrange("p j (c i) -> p c j i", i=4)
+            if on_vector:
+                nc.vector.tensor_copy(dst, src)
+            else:
+                nc.scalar.activation(dst, src, ACT.Copy, scale=sign)
+
+        quant = {}
+
+        def quantise_weights(t):
+            for name in ("w1", "w3"):
+                if name == "w3":
+                    grouped = work.tile([P, PASSES * 512], BF16, name="grouped3", tag="after_w3", align_bytes=64, bufs=1)
+                else:
+                    grouped = work.tile([P, PASSES * 512], BF16, name="grouped1", align_bytes=64)
+                for a in range(PASSES):
+                    interleave(grouped[:, a * 512:(a + 1) * 512], raw[(name, t, a)][:],
+                               sign=-1.0 if name == "w1" else 1.0, on_vector=(name == "w3" and t == 0))
+                codes = keep.tile([P, PASSES * P], U32, name="codes_%s_%d" % (name, t), align_bytes=64)
+                scales = keep.tile([P, PASSES * P], U8, name="scales_%s_%d" % (name, t), align_bytes=64)
+                nc.vector.quantize_mx(out=codes[:].bitcast(FP8X4), scales=scales[:], in_=grouped[:])
+                quant[(name, t)] = (codes, scales)
+
+        def weight_operand(name, t, a):
+            if name == "w2":
+                first = a * H + t * P
+                return w2_w[:, 2 * first:2 * (first + P)].bitcast(FP4X4), w2_sc[:, first:first + P]
+            codes, scales = quant[(name, t)]
+            return codes[:, a * P:(a + 1) * P].bitcast(FP8X4), scales[:, a * P:(a + 1) * P]
+
+        def first_product(names, c, tag, bufs):
+            t, hf = divmod(c, 2)
+            bank = psum.tile([P, HALF], F32, name=tag, tag=tag, bufs=bufs)
+            terms = [(name, a) for name in names for a in range(PASSES)]
+            width = HALF if c == 0 else P
+            for j0 in range(0, HALF, width):
+                for i, (name, a) in enumerate(terms):
+                    w_codes, w_plane = weight_operand(name, t, a)
+                    v_codes = v_w[(a, hf)][:, j0:j0 + width].bitcast(FP8X4)
+                    first = a * S + hf * HALF + j0
+                    v_plane = v_planes[:, first:first + width]
+                    flags = dict(start=(i == 0), stop=(i == len(terms) - 1))
+                    if c == 0:
+                        nc.tensor.matmul_mx(out=bank[:], lhsT=w_codes, lhsT_scale=w_plane,
+                                            rhs=v_codes, rhs_scale=v_plane, **flags)
+                    else:
+                        nc.tensor.matmul_mx(out=bank[:, j0:j0 + P], lhsT=v_codes, lhsT_scale=v_plane,
+                                            rhs=w_codes, rhs_scale=w_plane, **flags)
+            return bank
+
+        def difference(c):
+            bank_b = first_product(["w2"], c, "bank_b", 1)
+            b_sb = work.tile([P, HALF], F32, name="b_sb", tag="b_sb", bufs=3)
+            if c % 2 == 0:
+                dist = work.tile([P, HALF], F32, name="dist_even", tag="after_gate", align_bytes=64, bufs=1)
+            else:
+                dist = work.tile([P, HALF], F32, name="dist_odd", bufs=1)
+            if c in SUMMED_IN_PSUM:
+                bank_a = first_product(["w2", "w1"], c, "bank_a", 2)
+                nc.scalar.activation(dist[:], bank_a[:], ACT.Abs)
+                nc.scalar.copy(b_sb[:], bank_b[:])
+            else:
+                bank_a = first_product(["w1"], c, "bank_a", 2)
+                nc.scalar.copy(b_sb[:], bank_b[:])
+                diff = work.tile([P, HALF], F32, name="diff")
+                nc.vector.tensor_tensor(diff[:], bank_a[:], b_sb[:], ALU.add)
+                nc.scalar.activation(dist[:], diff[:], ACT.Abs)
+            return dist, b_sb
+
+        def gate(dist, bank_c):
+            prod = work.tile([P, HALF], F32, name="prod")
+            nc.vector.tensor_tensor(prod[:], bank_c[:], dist[:], ALU.mult)
+            return prod
+
+        def turn_and_add(prod, b_sb):
+            bank_h = psum.tile([P, HALF], F32, name="bank_h", tag="bank_h", bufs=1)
+            for b in range(BLOCKS):
+                cols = slice(b * P, (b + 1) * P)
+                nc.tensor.matmul(bank_h[:, cols], lhsT=b_sb[:, cols], rhs=ident32[:],
+                                 start=True, stop=False, is_transpose=True)
+                nc.tensor.matmul(bank_h[:, cols], lhsT=prod[:, cols], rhs=ident32[:],
+                                 start=False, stop=True, is_transpose=True)
+            h_sb = work.tile([P, HALF], F32, name="h_sb", tag="h_sb", bufs=3)
+            nc.scalar.copy(h_sb[:], bank_h[:])
+            return h_sb
+
+        x_turned = [keep.tile([P, BLOCKS, 2, P], F32, name="x_turned%d" % hf) for hf in range(2)]
+
+        def reread(t, hf):
+            picked = work.tile([P, HALF], F32, name="picked", tag=("after_w3", "after_gate")[hf],
+                               align_bytes=64, bufs=1)
+            nc.vector.tensor_copy(picked[:], page[t][:].indirect(half_list(list3, hf)))
+            x_rows = work.tile([P, HALF], BF16, name="x_rows")
+            nc.scalar.activation(x_rows[:], picked[:], ACT.Copy, scale=sc_col[:, t:t + 1])
+            bank_x = psum.tile([P, HALF], BF16, name="bank_x", tag="bank_x", bufs=2)
+            for b in range(BLOCKS):
+                cols = slice(b * P, (b + 1) * P)
+                nc.tensor.transpose(bank_x[:, cols], x_rows[:, cols], ident16[:])
+            nc.scalar.copy(
+                x_turned[hf][:, :, :, 32 * t:32 * (t + 1)],
+                bank_x[:].bitcast(F32).rearrange("m (b q u) -> m b u q", b=BLOCKS, u=2),
+            )
+
+        chunks = 2 * TILES
+        quantise_weights(0)
+        dist, b_sb = difference(0)
+        bank_c = first_product(["w3"], 0, "bank_c", 2)
+        for c in range(chunks):
+            t, hf = divmod(c, 2)
+            prod = gate(dist, bank_c)
+            b_prev = b_sb
+            if t > 0 and hf == 1:
+                reread(t - 1, 1)
+            if c + 1 < chunks:
+                dist, b_sb = difference(c + 1)
+            if c == 0:
+                h_sb = work.tile([P, HALF], F32, name="h_sb", tag="h_sb", bufs=3)
+                nc.vector.tensor_tensor(h_sb[:], prod[:], b_prev[:], ALU.add)
+            else:
+                h_sb = turn_and_add(prod, b_prev)
+            if c + 1 < chunks:
+                bank_c = first_product(["w3"], c + 1, "bank_c", 2)
+            if t > 0 and hf == 0:
+                reread(t - 1, 0)
+            nc.vector.tensor_tensor(
+                page[t][:].indirect(half_list(list2, hf)), h_sb[:], wgs_half[hf][:], ALU.mult
+            )
+            if hf == 0 and t + 1 < TILES:
+                quantise_weights(t + 1)
+            if c == chunks - 2:
+                grouped4 = keep.tile([P, PACK * H], BF16, name="grouped4", align_bytes=64)
+                interleave(grouped4[:], raw_w4[:])
+                w4_codes = keep.tile([P, H], U32, name="w4_codes", align_bytes=64)
+                w4_sc = keep.tile([P, H], U8, name="w4_sc", align_bytes=64)
+                nc.vector.quantize_mx(out=w4_codes[:].bitcast(FP8X4), scales=w4_sc[:], in_=grouped4[:])
+
+        def quantise_x(hf):
+            x_grouped = keep.tile([P, PACK * HALF], BF16, name="x_grouped%d" % hf,
+                                  tag="x_grouped%d" % hf, align_bytes=64)
+            for pair in range(2):
+                bank_x = psum.tile([P, HALF], F32, name="bank_x", tag="bank_x", bufs=2)
+                for b in range(2):
+                    for u in range(2):
+                        cols = slice((2 * b + u) * P, (2 * b + u + 1) * P)
+                        nc.tensor.transpose(bank_x[:, cols], x_turned[hf][:, 2 * pair + b, u, :], ident32[:])
+                nc.scalar.copy(
+                    x_grouped[:, pair * 1024:(pair + 1) * 1024].bitcast(F32).rearrange(
+                        "p (b m u) -> p b m u", b=2, u=2),
+                    bank_x[:].rearrange("p (b u m) -> p b m u", b=2, u=2),
+                )
+            codes = keep.tile([P, HALF], U32, name="x_codes%d" % hf, align_bytes=64)
+            scales = keep.tile([P, HALF], U8, name="x_scales%d" % hf, align_bytes=64)
+            nc.vector.quantize_mx(out=codes[:].bitcast(FP8X4), scales=scales[:], in_=x_grouped[:])
+            return codes, scales
+
+        def same_field(hf, tag, align):
+            picked = keep.tile([P, TILES, HALF], F32, name="field%d" % hf, tag=tag, align_bytes=align)
+            for t in range(TILES):
+                nc.vector.tensor_copy(picked[:, t, :], page[t][:].indirect(half_list(list4, hf)))
+            return picked
+
+        reread(TILES - 1, 0)
+        reread(TILES - 1, 1)
+        x_quant = [quantise_x(0), quantise_x(1)]
+        field = [same_field(0, "after_scatter", None), same_field(1, "x_grouped0", 64)]
+
+        def second_products(hf, t):
+            codes, scales = x_quant[hf]
+            rows = slice(t * P, (t + 1) * P)
+            bank_p = psum.tile([P, HALF], F32, name="bank_p", tag="bank_a", bufs=2)
+            nc.tensor.matmul_mx(
+                out=bank_p[:], lhsT=w4_codes[:, rows].bitcast(FP8X4), lhsT_scale=w4_sc[:, rows],
+                rhs=codes[:].bitcast(FP8X4), rhs_scale=scales[:], start=True, stop=True,
+            )
+            bank_q = psum.tile([P, HALF], F32, name="bank_q", tag="bank_c", bufs=2)
+            nc.tensor.matmul_mx(
+                out=bank_q[:], lhsT=w5_w[:, rows].bitcast(FP8X4), lhsT_scale=w5_sc[:, rows],
+                rhs=codes[:].bitcast(FP8X4), rhs_scale=scales[:], start=True, stop=True,
+            )
+            squashed = work.tile([P, HALF], F32, name="squashed", tag="b_sb", bufs=3)
+            nc.scalar.activation(squashed[:], bank_p[:], ACT.Tanh)
+            y_sb = work.tile([P, HALF], F32, name="y_sb", tag="h_sb", bufs=3)
+            nc.vector.tensor_tensor(y_sb[:], bank_q[:], squashed[:], ALU.mult)
+            return y_sb
+
+        def finish(hf, t, y_sb):
+            result = work.tile([P, HALF], F32, name="result", bufs=4)
+            nc.vector.scalar_tensor_tensor(
+                result[:], field[hf][:, t, :], gf_col[:, t:t + 1], y_sb[:], ALU.mult, ALU.add
+            )
+            nc.sync.dma_start(out=out[t * P:(t + 1) * P, hf * HALF:(hf + 1) * HALF], in_=result[:])
+
+        steps = [(hf, t) for hf in range(2) for t in range(TILES)]
+        y_next = second_products(*steps[0])
+        for i, step in enumerate(steps):
+            y_sb = y_next
+            if i + 1 < len(steps):
+                y_next = second_products(*steps[i + 1])
+            finish(step[0], step[1], y_sb)

@@ -59,8 +59,6 @@ def tile_list_lint_classing_step_kernel(
                 out=w2_sc[32 * q:32 * q + 4, :].bitcast(I32).rearrange("r (a c) -> r a c", a=PASSES),
                 in_=w2_scales[:, 4 * q:4 * q + 4, :].bitcast(I32).rearrange("a r c -> r a c"),
             )
-        v_planes = keep.tile([P, PASSES * S], U8, name="v_planes", align_bytes=64)
-        nc.vector.memset(v_planes[:].bitcast(I32), 0)
         w5_sc = keep.tile([P, H], U8, name="w5_sc", align_bytes=64)
         nc.vector.memset(w5_sc[:].bitcast(I32), 0)
 
@@ -76,24 +74,28 @@ def tile_list_lint_classing_step_kernel(
 
         list1 = load_list(offs, "list1")
         tab_w = []
-        for a in range(PASSES):
-            tile = keep.tile([P, T], U32, name="tab_w%d" % a)
+
+        def load_table(a):
+            tile = keep.tile([P, T], U32, name="tab_w%d" % a, tag="tab_w%d" % a, align_bytes=64)
             nc.sync.dma_start(
                 out=tile[:].bitcast(I32), in_=tab_words[a].rearrange("p n i -> p (n i)").bitcast(I32)
             )
             tab_w.append(tile)
+
+        load_table(0)
         w2_w = keep.tile([P, PASSES * 2 * H], U8, name="w2_w", align_bytes=64)
         nc.sync.dma_start(
             out=w2_w[:].bitcast(I32).rearrange("p (a n) -> p a n", a=PASSES),
             in_=w2_words.bitcast(I32).rearrange("a p n -> p a n"),
         )
+        load_table(1)
 
         raw = {}
 
         def load_weights(t):
             for name, w in (("w1", w1), ("w3", w3)):
                 for a in range(PASSES):
-                    tile = keep.tile([P, PACK, P], F32, name="raw_%s_%d_%d" % (name, t, a))
+                    tile = keep.tile([P, PACK, P], F32, name="raw", tag="raw_%s_%d_%d" % (name, t, a))
                     nc.sync.dma_start(
                         out=tile[:],
                         in_=w[a * 512:(a + 1) * 512, t * P:(t + 1) * P].rearrange("(p j) c -> p j c", j=PACK),
@@ -143,18 +145,29 @@ def tile_list_lint_classing_step_kernel(
 
         v_sc = keep.tile([P, S], U8, name="v_sc", align_bytes=64)
         nc.vector.tensor_copy(v_sc[:], tab_sc[:].indirect(list1[:]))
-        for a in range(PASSES):
+        v_w = {}
+        v_planes = []
+
+        def place_plane(a, tag):
+            plane = keep.tile([P, S], U8, name="v_plane%d" % a, tag=tag, align_bytes=64)
+            nc.vector.memset(plane[:].bitcast(I32), 0)
             for q in range(4):
                 nc.scalar.dma_start(
-                    out=v_planes[32 * q:32 * q + 4, a * S:(a + 1) * S].bitcast(I32),
+                    out=plane[32 * q:32 * q + 4, :].bitcast(I32),
                     in_=v_sc[16 * a + 4 * q:16 * a + 4 * q + 4, :].bitcast(I32),
                 )
-        v_w = {}
-        for a in range(PASSES):
+            v_planes.append(plane)
+
+        def gather_words(a):
             for hf in range(2):
                 tile = keep.tile([P, HALF], U32, name="v_w%d_%d" % (a, hf), align_bytes=64)
                 nc.vector.tensor_copy(tile[:], tab_w[a][:].indirect(half_list(list1, hf)))
                 v_w[(a, hf)] = tile
+
+        place_plane(0, "v_plane0")
+        gather_words(0)
+        place_plane(1, "tab_w0")
+        gather_words(1)
 
         def interleave(dst, src, sign=1.0, on_vector=False):
             dst = dst.rearrange("p (c i j) -> p c j i", i=4, j=PACK)
@@ -171,7 +184,7 @@ def tile_list_lint_classing_step_kernel(
                 if name == "w3":
                     grouped = work.tile([P, PASSES * 512], BF16, name="grouped3", tag="after_w3", align_bytes=64, bufs=1)
                 else:
-                    grouped = work.tile([P, PASSES * 512], BF16, name="grouped1", align_bytes=64)
+                    grouped = work.tile([P, PASSES * 512], BF16, name="grouped1", tag="after_w1", align_bytes=64, bufs=1)
                 for a in range(PASSES):
                     interleave(grouped[:, a * 512:(a + 1) * 512], raw[(name, t, a)][:],
                                sign=-1.0 if name == "w1" else 1.0, on_vector=(name == "w3" and t == 0))
@@ -196,8 +209,8 @@ def tile_list_lint_classing_step_kernel(
                 for i, (name, a) in enumerate(terms):
                     w_codes, w_plane = weight_operand(name, t, a)
                     v_codes = v_w[(a, hf)][:, j0:j0 + width].bitcast(FP8X4)
-                    first = a * S + hf * HALF + j0
-                    v_plane = v_planes[:, first:first + width]
+                    first = hf * HALF + j0
+                    v_plane = v_planes[a][:, first:first + width]
                     flags = dict(start=(i == 0), stop=(i == len(terms) - 1))
                     if c == 0:
                         nc.tensor.matmul_mx(out=bank[:], lhsT=w_codes, lhsT_scale=w_plane,
@@ -231,7 +244,7 @@ def tile_list_lint_classing_step_kernel(
             nc.vector.tensor_tensor(prod[:], bank_c[:], dist[:], ALU.mult)
             return prod
 
-        def turn_and_add(prod, b_sb):
+        def turn_and_add(c, prod, b_sb):
             bank_h = psum.tile([P, HALF], F32, name="bank_h", tag="bank_h", bufs=1)
             for b in range(BLOCKS):
                 cols = slice(b * P, (b + 1) * P)
@@ -239,11 +252,16 @@ def tile_list_lint_classing_step_kernel(
                                  start=True, stop=False, is_transpose=True)
                 nc.tensor.matmul(bank_h[:, cols], lhsT=prod[:, cols], rhs=ident32[:],
                                  start=False, stop=True, is_transpose=True)
-            h_sb = work.tile([P, HALF], F32, name="h_sb", tag="h_sb", bufs=3)
+            if c == 1:
+                h_sb = work.tile([P, HALF], F32, name="h_second", tag="after_w1", align_bytes=64, bufs=1)
+            else:
+                h_sb = work.tile([P, HALF], F32, name="h_sb", tag="h_sb", bufs=3)
             nc.scalar.copy(h_sb[:], bank_h[:])
             return h_sb
 
-        x_turned = [keep.tile([P, BLOCKS, 2, P], F32, name="x_turned%d" % hf) for hf in range(2)]
+        x_turned = [
+            keep.tile([P, BLOCKS, 2, P], F32, name="x_turned", tag="x_turned%d" % hf) for hf in range(2)
+        ]
 
         def reread(t, hf):
             picked = work.tile([P, HALF], F32, name="picked", tag=("after_w3", "after_gate")[hf],
@@ -276,7 +294,7 @@ def tile_list_lint_classing_step_kernel(
                 h_sb = work.tile([P, HALF], F32, name="h_sb", tag="h_sb", bufs=3)
                 nc.vector.tensor_tensor(h_sb[:], prod[:], b_prev[:], ALU.add)
             else:
-                h_sb = turn_and_add(prod, b_prev)
+                h_sb = turn_and_add(c, prod, b_prev)
             if c + 1 < chunks:
                 bank_c = first_product(["w3"], c + 1, "bank_c", 2)
             if t > 0 and hf == 0:
@@ -323,36 +341,51 @@ def tile_list_lint_classing_step_kernel(
         x_quant = [quantise_x(0), quantise_x(1)]
         field = [same_field(0, "after_scatter", None), same_field(1, "x_grouped0", 64)]
 
+        spare = [key for key in raw]
+
+        def spare_tile(name, i):
+            w_name, t, a = spare[i]
+            return keep.tile([P, HALF], F32, name=name, tag="raw_%s_%d_%d" % (w_name, t, a))
+
         def second_products(hf, t):
             codes, scales = x_quant[hf]
             rows = slice(t * P, (t + 1) * P)
-            bank_p = psum.tile([P, HALF], F32, name="bank_p", tag="bank_a", bufs=2)
+            tag_p, bufs_p = (("bank_a", 2), ("bank_a", 2), ("bank_b", 1), ("bank_x", 2))[t]
+            tag_q, bufs_q = (("bank_c", 2), ("bank_c", 2), ("bank_h", 1), ("bank_x", 2))[t]
+            bank_p = psum.tile([P, HALF], F32, name="bank_p", tag=tag_p, bufs=bufs_p)
             nc.tensor.matmul_mx(
                 out=bank_p[:], lhsT=w4_codes[:, rows].bitcast(FP8X4), lhsT_scale=w4_sc[:, rows],
                 rhs=codes[:].bitcast(FP8X4), rhs_scale=scales[:], start=True, stop=True,
             )
-            bank_q = psum.tile([P, HALF], F32, name="bank_q", tag="bank_c", bufs=2)
+            bank_q = psum.tile([P, HALF], F32, name="bank_q", tag=tag_q, bufs=bufs_q)
             nc.tensor.matmul_mx(
                 out=bank_q[:], lhsT=w5_w[:, rows].bitcast(FP8X4), lhsT_scale=w5_sc[:, rows],
                 rhs=codes[:].bitcast(FP8X4), rhs_scale=scales[:], start=True, stop=True,
             )
-            squashed = work.tile([P, HALF], F32, name="squashed", tag="b_sb", bufs=3)
+            if (hf, t) == (1, TILES - 1):
+                squashed = keep.tile([P, HALF], F32, name="squashed_last", tag="after_products")
+            else:
+                squashed = spare_tile("squashed", 3 * TILES + t)
             nc.scalar.activation(squashed[:], bank_p[:], ACT.Tanh)
-            y_sb = work.tile([P, HALF], F32, name="y_sb", tag="h_sb", bufs=3)
+            y_sb = spare_tile("y_sb", hf * TILES + t)
             nc.vector.tensor_tensor(y_sb[:], bank_q[:], squashed[:], ALU.mult)
             return y_sb
 
-        def finish(hf, t, y_sb):
-            result = work.tile([P, HALF], F32, name="result", bufs=4)
-            nc.vector.scalar_tensor_tensor(
-                result[:], field[hf][:, t, :], gf_col[:, t:t + 1], y_sb[:], ALU.mult, ALU.add
-            )
-            nc.sync.dma_start(out=out[t * P:(t + 1) * P, hf * HALF:(hf + 1) * HALF], in_=result[:])
+        def store(hf, t, result):
+            nc.sync.dma_start(out=out[t * P:(t + 1) * P, hf * HALF:(hf + 1) * HALF], in_=result)
 
-        steps = [(hf, t) for hf in range(2) for t in range(TILES)]
-        y_next = second_products(*steps[0])
-        for i, step in enumerate(steps):
-            y_sb = y_next
-            if i + 1 < len(steps):
-                y_next = second_products(*steps[i + 1])
-            finish(step[0], step[1], y_sb)
+        scaled = keep.tile([P, TILES, HALF], F32, name="scaled", tag="x_turned1")
+        for t in range(TILES):
+            nc.scalar.activation(scaled[:, t, :], field[0][:, t, :], ACT.Copy, scale=gf_col[:, t:t + 1])
+        for t in range(TILES):
+            y_sb = second_products(0, t)
+            result = spare_tile("result", 2 * TILES + t)
+            nc.gpsimd.tensor_tensor(result[:], scaled[:, t, :], y_sb[:], ALU.add)
+            store(0, t, result[:])
+        y_late = [second_products(1, t) for t in range(TILES)]
+        results = keep.tile([P, TILES, HALF], F32, name="results", tag="after_products")
+        for t in range(TILES):
+            nc.vector.scalar_tensor_tensor(
+                results[:, t, :], field[1][:, t, :], gf_col[:, t:t + 1], y_late[t][:], ALU.mult, ALU.add
+            )
+            store(1, t, results[:, t, :])

@@ -19,12 +19,15 @@ ACT = mybir.ActivationFunctionType
 
 P = 128
 PACK = 4
-PASSES = K // (P * PACK)
+K_PASS = P * PACK
+PASSES = K // K_PASS
+QUADS = 4
 TILES = H // P
 HALF = 512
 BLOCKS = HALF // P
-COLS = HALF // 16
-SUMMED_IN_PSUM = (2, 4, 6)
+LIST_COLS = HALF // 16
+CHUNKS = 2 * TILES
+AHEAD = 3
 
 
 def tile_list_lint_classing_step_kernel(
@@ -43,24 +46,28 @@ def tile_list_lint_classing_step_kernel(
             nc.sync.dma_start(tile[:], src)
             return tile
 
-        def half_list(tile, hf):
-            return tile[:, hf * COLS:(hf + 1) * COLS]
+        def half_list(tile, half):
+            return tile[:, half * LIST_COLS:(half + 1) * LIST_COLS]
+
+        def zeroed_plane(tag, width, engine):
+            plane = keep.tile([P, width], U8, name="plane", tag=tag, align_bytes=64)
+            engine.memset(plane[:].bitcast(I32), 0)
+            return plane
 
         tab_sc = keep.tile([P, T], U8, name="tab_sc", align_bytes=64)
         nc.sync.dma_start(
-            out=tab_sc[0:32, :].bitcast(I32), in_=tab_scales.rearrange("a q n -> (a q) n").bitcast(I32)
+            out=tab_sc[0:32, :].bitcast(I32), in_=tab_scales.rearrange("a g n -> (a g) n").bitcast(I32)
         )
         nc.vector.memset(tab_sc[32:64, :].bitcast(I32), 0)
         nc.vector.memset(tab_sc[64:P, :].bitcast(I32), 0)
-        w2_sc = keep.tile([P, PASSES * H], U8, name="w2_sc", align_bytes=64)
-        nc.gpsimd.memset(w2_sc[:].bitcast(I32), 0)
-        for q in range(4):
+
+        w2_sc = zeroed_plane("w2_sc", PASSES * H, nc.gpsimd)
+        for q in range(QUADS):
             nc.scalar.dma_start(
-                out=w2_sc[32 * q:32 * q + 4, :].bitcast(I32).rearrange("r (a c) -> r a c", a=PASSES),
-                in_=w2_scales[:, 4 * q:4 * q + 4, :].bitcast(I32).rearrange("a r c -> r a c"),
+                out=w2_sc[32 * q:32 * q + 4, :].bitcast(I32).rearrange("g (a c) -> g a c", a=PASSES),
+                in_=w2_scales[:, 4 * q:4 * q + 4, :].bitcast(I32).rearrange("a g c -> g a c"),
             )
-        w5_sc = keep.tile([P, H], U8, name="w5_sc", align_bytes=64)
-        nc.vector.memset(w5_sc[:].bitcast(I32), 0)
+        w5_sc = zeroed_plane("w5_sc", H, nc.vector)
 
         warm_in = keep.tile([P, 1], F32, name="warm_in")
         nc.vector.memset(warm_in[:], 0.0)
@@ -72,34 +79,26 @@ def tile_list_lint_classing_step_kernel(
         ident16 = keep.tile([P, P], BF16, name="ident16")
         make_identity(nc, ident16[:])
 
-        list1 = load_list(offs, "list1")
         tab_w = []
 
         def load_table(a):
-            tile = keep.tile([P, T], U32, name="tab_w%d" % a, tag="tab_w%d" % a, align_bytes=64)
+            tile = keep.tile([P, T], U32, name="tab_w", tag="tab_w%d" % a, align_bytes=64)
             nc.sync.dma_start(
                 out=tile[:].bitcast(I32), in_=tab_words[a].rearrange("p n i -> p (n i)").bitcast(I32)
             )
             tab_w.append(tile)
 
-        load_table(0)
-        w2_w = keep.tile([P, PASSES * 2 * H], U8, name="w2_w", align_bytes=64)
-        nc.sync.dma_start(
-            out=w2_w[:].bitcast(I32).rearrange("p (a n) -> p a n", a=PASSES),
-            in_=w2_words.bitcast(I32).rearrange("a p n -> p a n"),
-        )
-        load_table(1)
-
         raw = {}
+
+        def raw_tag(name, t, a):
+            return "raw_%s_%d_%d" % (name, t, a)
 
         def load_weights(t):
             for name, w in (("w1", w1), ("w3", w3)):
                 for a in range(PASSES):
-                    tile = keep.tile([P, PACK, P], F32, name="raw", tag="raw_%s_%d_%d" % (name, t, a))
-                    nc.sync.dma_start(
-                        out=tile[:],
-                        in_=w[a * 512:(a + 1) * 512, t * P:(t + 1) * P].rearrange("(p j) c -> p j c", j=PACK),
-                    )
+                    tile = keep.tile([P, PACK, P], F32, name="raw", tag=raw_tag(name, t, a))
+                    rows = w[a * K_PASS:(a + 1) * K_PASS, t * P:(t + 1) * P]
+                    nc.sync.dma_start(out=tile[:], in_=rows.rearrange("(p i) c -> p i c", i=PACK))
                     raw[(name, t, a)] = tile
 
         page = []
@@ -109,89 +108,89 @@ def tile_list_lint_classing_step_kernel(
             nc.sync.dma_start(out=tile[:], in_=page0[t * P:(t + 1) * P, :])
             page.append(tile)
 
+        def load_row_values(src, name):
+            tile = keep.tile([P, TILES], F32, name=name)
+            with nc.allow_non_contiguous_dma(reason="one value for each row of a tile"):
+                nc.sync.dma_start(out=tile[:], in_=src.rearrange("(t p) -> p t", p=P))
+            return tile
+
+        list1 = load_list(offs, "list1")
+        load_table(0)
+        w2_w = keep.tile([P, PASSES * 2 * H], U8, name="w2_w", align_bytes=64)
+        nc.sync.dma_start(
+            out=w2_w[:].bitcast(I32).rearrange("p (a n) -> p a n", a=PASSES),
+            in_=w2_words.bitcast(I32).rearrange("a p n -> p a n"),
+        )
+        load_table(1)
         load_weights(0)
         list2 = load_list(offs2, "list2")
         wgs0 = keep.tile([P, HALF], F32, name="wgs0")
         nc.sync.dma_start(out=wgs0[:], in_=wgs[:, 0:HALF])
         load_page(0)
-        wgs1 = keep.tile([P, HALF], F32, name="wgs1", tag="after_scatter")
-        nc.sync.dma_start(out=wgs1[:], in_=wgs[:, HALF:S])
-        wgs_half = [wgs0, wgs1]
         load_weights(1)
         list3 = load_list(offs3, "list3")
-        sc_col = keep.tile([P, TILES], F32, name="sc_col")
-        gf_col = keep.tile([P, TILES], F32, name="gf_col")
-        with nc.allow_non_contiguous_dma(reason="one value for each row of a tile"):
-            nc.sync.dma_start(out=sc_col[:], in_=sc.rearrange("(t p) -> p t", p=P))
         load_weights(2)
+        wgs1 = keep.tile([P, HALF], F32, name="wgs1", tag="after_scatters")
+        nc.sync.dma_start(out=wgs1[:], in_=wgs[:, HALF:S])
+        wgs_half = [wgs0, wgs1]
+        sc_col = load_row_values(sc, "sc_col")
         load_page(1)
         load_weights(3)
         load_page(2)
         load_page(3)
         raw_w4 = keep.tile([P, PACK, H], F32, name="raw_w4")
-        nc.sync.dma_start(out=raw_w4[:], in_=w4.rearrange("(p j) c -> p j c", j=PACK))
+        nc.sync.dma_start(out=raw_w4[:], in_=w4.rearrange("(p i) c -> p i c", i=PACK))
         w5_w = keep.tile([P, H], U32, name="w5_w", align_bytes=64)
         nc.sync.dma_start(
             out=w5_w[:].bitcast(I32), in_=w5_words[0].rearrange("p n i -> p (n i)").bitcast(I32)
         )
-        for q in range(4):
+        for q in range(QUADS):
             nc.sync.dma_start(
                 out=w5_sc[32 * q:32 * q + 4, :].bitcast(I32),
                 in_=w5_scales[0, 4 * q:4 * q + 4, :].bitcast(I32),
             )
         list4 = load_list(offs4, "list4")
-        with nc.allow_non_contiguous_dma(reason="one value for each row of a tile"):
-            nc.sync.dma_start(out=gf_col[:], in_=gf.rearrange("(t p) -> p t", p=P))
+        gf_col = load_row_values(gf, "gf_col")
 
         v_sc = keep.tile([P, S], U8, name="v_sc", align_bytes=64)
         nc.vector.tensor_copy(v_sc[:], tab_sc[:].indirect(list1[:]))
-        v_w = {}
         v_planes = []
-
-        def place_plane(a, tag):
-            plane = keep.tile([P, S], U8, name="v_plane%d" % a, tag=tag, align_bytes=64)
-            nc.vector.memset(plane[:].bitcast(I32), 0)
-            for q in range(4):
+        v_w = {}
+        for a, tag in enumerate(("v_plane0", "tab_w0")):
+            plane = zeroed_plane(tag, S, nc.vector)
+            for q in range(QUADS):
                 nc.scalar.dma_start(
                     out=plane[32 * q:32 * q + 4, :].bitcast(I32),
                     in_=v_sc[16 * a + 4 * q:16 * a + 4 * q + 4, :].bitcast(I32),
                 )
             v_planes.append(plane)
+            for half in range(2):
+                tile = keep.tile([P, HALF], U32, name="v_w%d_%d" % (a, half), align_bytes=64)
+                nc.vector.tensor_copy(tile[:], tab_w[a][:].indirect(half_list(list1, half)))
+                v_w[(a, half)] = tile
 
-        def gather_words(a):
-            for hf in range(2):
-                tile = keep.tile([P, HALF], U32, name="v_w%d_%d" % (a, hf), align_bytes=64)
-                nc.vector.tensor_copy(tile[:], tab_w[a][:].indirect(half_list(list1, hf)))
-                v_w[(a, hf)] = tile
+        def interleave_views(dst, src):
+            return (dst.rearrange("p (c n i) -> p c i n", n=4, i=PACK),
+                    src.rearrange("p i (c n) -> p c i n", n=4))
 
-        place_plane(0, "v_plane0")
-        gather_words(0)
-        place_plane(1, "tab_w0")
-        gather_words(1)
-
-        def interleave(dst, src, sign=1.0, on_vector=False):
-            dst = dst.rearrange("p (c i j) -> p c j i", i=4, j=PACK)
-            src = src.rearrange("p j (c i) -> p c j i", i=4)
-            if on_vector:
-                nc.vector.tensor_copy(dst, src)
-            else:
-                nc.scalar.activation(dst, src, ACT.Copy, scale=sign)
+        def quantise(name, grouped, width):
+            codes = keep.tile([P, width], U32, name="codes_" + name, align_bytes=64)
+            scales = keep.tile([P, width], U8, name="scales_" + name, align_bytes=64)
+            nc.vector.quantize_mx(out=codes[:].bitcast(FP8X4), scales=scales[:], in_=grouped[:])
+            return codes, scales
 
         quant = {}
 
         def quantise_weights(t):
-            for name in ("w1", "w3"):
-                if name == "w3":
-                    grouped = work.tile([P, PASSES * 512], BF16, name="grouped3", tag="after_w3", align_bytes=64, bufs=1)
-                else:
-                    grouped = work.tile([P, PASSES * 512], BF16, name="grouped1", tag="after_w1", align_bytes=64, bufs=1)
+            for name, sign in (("w1", -1.0), ("w3", 1.0)):
+                grouped = work.tile([P, PASSES * K_PASS], BF16, name="grouped", align_bytes=64, bufs=3)
                 for a in range(PASSES):
-                    interleave(grouped[:, a * 512:(a + 1) * 512], raw[(name, t, a)][:],
-                               sign=-1.0 if name == "w1" else 1.0, on_vector=(name == "w3" and t == 0))
-                codes = keep.tile([P, PASSES * P], U32, name="codes_%s_%d" % (name, t), align_bytes=64)
-                scales = keep.tile([P, PASSES * P], U8, name="scales_%s_%d" % (name, t), align_bytes=64)
-                nc.vector.quantize_mx(out=codes[:].bitcast(FP8X4), scales=scales[:], in_=grouped[:])
-                quant[(name, t)] = (codes, scales)
+                    dst, src = interleave_views(grouped[:, a * K_PASS:(a + 1) * K_PASS], raw[(name, t, a)][:])
+                    if (name, t, a) == ("w3", 0, PASSES - 1):
+                        nc.vector.tensor_copy(dst, src)
+                    else:
+                        nc.scalar.activation(dst, src, ACT.Copy, scale=sign)
+                quant[(name, t)] = quantise("%s_%d" % (name, t), grouped, PASSES * P)
 
         def weight_operand(name, t, a):
             if name == "w2":
@@ -200,19 +199,24 @@ def tile_list_lint_classing_step_kernel(
             codes, scales = quant[(name, t)]
             return codes[:, a * P:(a + 1) * P].bitcast(FP8X4), scales[:, a * P:(a + 1) * P]
 
-        def first_product(names, c, tag, bufs):
-            t, hf = divmod(c, 2)
-            bank = psum.tile([P, HALF], F32, name=tag, tag=tag, bufs=bufs)
+        bank_bufs = {"bank_a": 2, "bank_b": 1, "bank_c": 2, "bank_h": 1, "bank_x": 2}
+
+        def new_bank(tag, dtype=F32):
+            return psum.tile([P, HALF], dtype, name=tag, tag=tag, bufs=bank_bufs[tag])
+
+        def first_product(names, c, tag, by_rows):
+            t, half = divmod(c, 2)
+            bank = new_bank(tag)
             terms = [(name, a) for name in names for a in range(PASSES)]
-            width = HALF if c == 0 else P
+            width = HALF if by_rows else P
             for j0 in range(0, HALF, width):
                 for i, (name, a) in enumerate(terms):
                     w_codes, w_plane = weight_operand(name, t, a)
-                    v_codes = v_w[(a, hf)][:, j0:j0 + width].bitcast(FP8X4)
-                    first = hf * HALF + j0
+                    v_codes = v_w[(a, half)][:, j0:j0 + width].bitcast(FP8X4)
+                    first = half * HALF + j0
                     v_plane = v_planes[a][:, first:first + width]
                     flags = dict(start=(i == 0), stop=(i == len(terms) - 1))
-                    if c == 0:
+                    if by_rows:
                         nc.tensor.matmul_mx(out=bank[:], lhsT=w_codes, lhsT_scale=w_plane,
                                             rhs=v_codes, rhs_scale=v_plane, **flags)
                     else:
@@ -220,172 +224,166 @@ def tile_list_lint_classing_step_kernel(
                                             rhs=w_codes, rhs_scale=w_plane, **flags)
             return bank
 
+        def copied_out(bank, name, bufs):
+            tile = work.tile([P, HALF], F32, name=name, bufs=bufs)
+            nc.scalar.copy(tile[:], bank[:])
+            return tile
+
+        def magnitude(src):
+            dist = work.tile([P, HALF], F32, name="dist", bufs=AHEAD)
+            nc.scalar.activation(dist[:], src[:], ACT.Abs)
+            return dist
+
+        def subtracted(bank_a, b_sb):
+            diff = work.tile([P, HALF], F32, name="diff")
+            nc.vector.tensor_tensor(diff[:], bank_a[:], b_sb[:], ALU.add)
+            return magnitude(diff)
+
         def difference(c):
-            bank_b = first_product(["w2"], c, "bank_b", 1)
-            b_sb = work.tile([P, HALF], F32, name="b_sb", tag="b_sb", bufs=3)
+            bank_b = first_product(["w2"], c, "bank_b", False)
             if c % 2 == 0:
-                dist = work.tile([P, HALF], F32, name="dist_even", tag="after_gate", align_bytes=64, bufs=1)
-            else:
-                dist = work.tile([P, HALF], F32, name="dist_odd", bufs=1)
-            if c in SUMMED_IN_PSUM:
-                bank_a = first_product(["w2", "w1"], c, "bank_a", 2)
-                nc.scalar.activation(dist[:], bank_a[:], ACT.Abs)
-                nc.scalar.copy(b_sb[:], bank_b[:])
-            else:
-                bank_a = first_product(["w1"], c, "bank_a", 2)
-                nc.scalar.copy(b_sb[:], bank_b[:])
-                diff = work.tile([P, HALF], F32, name="diff")
-                nc.vector.tensor_tensor(diff[:], bank_a[:], b_sb[:], ALU.add)
-                nc.scalar.activation(dist[:], diff[:], ACT.Abs)
-            return dist, b_sb
+                dist = magnitude(first_product(["w2", "w1"], c, "bank_a", False))
+                return dist, copied_out(bank_b, "b_sb", AHEAD + 1)
+            bank_a = first_product(["w1"], c, "bank_a", False)
+            b_sb = copied_out(bank_b, "b_sb", AHEAD + 1)
+            return subtracted(bank_a, b_sb), b_sb
 
         def gate(dist, bank_c):
-            prod = work.tile([P, HALF], F32, name="prod")
+            prod = work.tile([P, HALF], F32, name="prod", bufs=4)
             nc.vector.tensor_tensor(prod[:], bank_c[:], dist[:], ALU.mult)
             return prod
 
-        def turn_and_add(c, prod, b_sb):
-            bank_h = psum.tile([P, HALF], F32, name="bank_h", tag="bank_h", bufs=1)
+        def new_tags(prod, b_sb):
+            bank = new_bank("bank_h")
             for b in range(BLOCKS):
                 cols = slice(b * P, (b + 1) * P)
-                nc.tensor.matmul(bank_h[:, cols], lhsT=b_sb[:, cols], rhs=ident32[:],
+                nc.tensor.matmul(bank[:, cols], lhsT=b_sb[:, cols], rhs=ident32[:],
                                  start=True, stop=False, is_transpose=True)
-                nc.tensor.matmul(bank_h[:, cols], lhsT=prod[:, cols], rhs=ident32[:],
+                nc.tensor.matmul(bank[:, cols], lhsT=prod[:, cols], rhs=ident32[:],
                                  start=False, stop=True, is_transpose=True)
-            if c == 1:
-                h_sb = work.tile([P, HALF], F32, name="h_second", tag="after_w1", align_bytes=64, bufs=1)
-            else:
-                h_sb = work.tile([P, HALF], F32, name="h_sb", tag="h_sb", bufs=3)
-            nc.scalar.copy(h_sb[:], bank_h[:])
-            return h_sb
+            return copied_out(bank, "h_sb", 4)
 
-        x_turned = [
-            keep.tile([P, BLOCKS, 2, P], F32, name="x_turned", tag="x_turned%d" % hf) for hf in range(2)
-        ]
+        def scatter(c, h_sb):
+            t, half = divmod(c, 2)
+            nc.vector.tensor_tensor(
+                page[t][:].indirect(half_list(list2, half)), h_sb[:], wgs_half[half][:], ALU.mult
+            )
 
-        def reread(t, hf):
-            picked = work.tile([P, HALF], F32, name="picked", tag=("after_w3", "after_gate")[hf],
-                               align_bytes=64, bufs=1)
-            nc.vector.tensor_copy(picked[:], page[t][:].indirect(half_list(list3, hf)))
+        x_turned = [keep.tile([P, BLOCKS, 2, P], F32, name="x_turned%d" % half) for half in range(2)]
+
+        def reread(t, half):
+            picked = work.tile([P, HALF], F32, name="picked")
+            nc.vector.tensor_copy(picked[:], page[t][:].indirect(half_list(list3, half)))
             x_rows = work.tile([P, HALF], BF16, name="x_rows")
             nc.scalar.activation(x_rows[:], picked[:], ACT.Copy, scale=sc_col[:, t:t + 1])
-            bank_x = psum.tile([P, HALF], BF16, name="bank_x", tag="bank_x", bufs=2)
+            bank_x = new_bank("bank_x", BF16)
             for b in range(BLOCKS):
                 cols = slice(b * P, (b + 1) * P)
                 nc.tensor.transpose(bank_x[:, cols], x_rows[:, cols], ident16[:])
             nc.scalar.copy(
-                x_turned[hf][:, :, :, 32 * t:32 * (t + 1)],
+                x_turned[half][:, :, :, 32 * t:32 * (t + 1)],
                 bank_x[:].bitcast(F32).rearrange("m (b q u) -> m b u q", b=BLOCKS, u=2),
             )
 
-        chunks = 2 * TILES
         quantise_weights(0)
-        dist, b_sb = difference(0)
-        bank_c = first_product(["w3"], 0, "bank_c", 2)
-        for c in range(chunks):
-            t, hf = divmod(c, 2)
-            prod = gate(dist, bank_c)
-            b_prev = b_sb
-            if t > 0 and hf == 1:
-                reread(t - 1, 1)
-            if c + 1 < chunks:
-                dist, b_sb = difference(c + 1)
-            if c == 0:
-                h_sb = work.tile([P, HALF], F32, name="h_sb", tag="h_sb", bufs=3)
-                nc.vector.tensor_tensor(h_sb[:], prod[:], b_prev[:], ALU.add)
-            else:
-                h_sb = turn_and_add(c, prod, b_prev)
-            if c + 1 < chunks:
-                bank_c = first_product(["w3"], c + 1, "bank_c", 2)
-            if t > 0 and hf == 0:
-                reread(t - 1, 0)
-            nc.vector.tensor_tensor(
-                page[t][:].indirect(half_list(list2, hf)), h_sb[:], wgs_half[hf][:], ALU.mult
-            )
-            if hf == 0 and t + 1 < TILES:
-                quantise_weights(t + 1)
-            if c == chunks - 2:
-                grouped4 = keep.tile([P, PACK * H], BF16, name="grouped4", align_bytes=64)
-                interleave(grouped4[:], raw_w4[:])
-                w4_codes = keep.tile([P, H], U32, name="w4_codes", align_bytes=64)
-                w4_sc = keep.tile([P, H], U8, name="w4_sc", align_bytes=64)
-                nc.vector.quantize_mx(out=w4_codes[:].bitcast(FP8X4), scales=w4_sc[:], in_=grouped4[:])
+        b_first = [
+            copied_out(first_product(["w2"], c, ("bank_b", "bank_h")[c], c == 0), "b_sb", AHEAD + 1)
+            for c in range(2)
+        ]
+        dist_first = [subtracted(first_product(["w1"], c, "bank_a", c == 0), b_first[c]) for c in range(2)]
+        prod_first = [gate(dist_first[c], first_product(["w3"], c, "bank_c", c == 0)) for c in range(2)]
+        h_first = work.tile([P, HALF], F32, name="h_first", bufs=1)
+        nc.vector.tensor_tensor(h_first[:], prod_first[0][:], b_first[0][:], ALU.add)
+        h_ready = {1: new_tags(prod_first[1], b_first[1])}
+        scatter(0, h_first)
+        quantise_weights(1)
+        fronts = {2: difference(2)}
+        banks_c = {2: first_product(["w3"], 2, "bank_c", False)}
+        fronts[3] = difference(3)
 
-        def quantise_x(hf):
-            x_grouped = keep.tile([P, PACK * HALF], BF16, name="x_grouped%d" % hf,
-                                  tag="x_grouped%d" % hf, align_bytes=64)
-            for pair in range(2):
-                bank_x = psum.tile([P, HALF], F32, name="bank_x", tag="bank_x", bufs=2)
+        for c in range(1, CHUNKS):
+            t, half = divmod(c, 2)
+            if half == 1 and t + 2 < TILES:
+                quantise_weights(t + 2)
+            if c + 1 < CHUNKS:
+                dist, b_sb = fronts[c + 1]
+                prod = gate(dist, banks_c[c + 1])
+                if c + 2 < CHUNKS:
+                    banks_c[c + 2] = first_product(["w3"], c + 2, "bank_c", False)
+                h_ready[c + 1] = new_tags(prod, b_sb)
+            if c + AHEAD < CHUNKS:
+                fronts[c + AHEAD] = difference(c + AHEAD)
+            if t > 0:
+                reread(t - 1, half)
+            scatter(c, h_ready[c])
+            if c == CHUNKS - 2:
+                grouped4 = keep.tile([P, PACK * H], BF16, name="grouped4", align_bytes=64)
+                dst, src = interleave_views(grouped4[:], raw_w4[:])
+                nc.scalar.activation(dst, src, ACT.Copy)
+                w4_codes, w4_sc = quantise("w4", grouped4, H)
+
+        def quantise_x(half):
+            x_grouped = keep.tile([P, PACK * HALF], BF16, name="x_grouped", tag="x_grouped%d" % half,
+                                  align_bytes=64)
+            words = x_grouped[:].bitcast(F32)
+            for pair in range(BLOCKS // 2):
+                bank_x = new_bank("bank_x")
                 for b in range(2):
                     for u in range(2):
                         cols = slice((2 * b + u) * P, (2 * b + u + 1) * P)
-                        nc.tensor.transpose(bank_x[:, cols], x_turned[hf][:, 2 * pair + b, u, :], ident32[:])
+                        nc.tensor.transpose(bank_x[:, cols], x_turned[half][:, 2 * pair + b, u, :], ident32[:])
                 nc.scalar.copy(
-                    x_grouped[:, pair * 1024:(pair + 1) * 1024].bitcast(F32).rearrange(
-                        "p (b m u) -> p b m u", b=2, u=2),
+                    words[:, pair * HALF:(pair + 1) * HALF].rearrange("p (b m u) -> p b m u", b=2, u=2),
                     bank_x[:].rearrange("p (b u m) -> p b m u", b=2, u=2),
                 )
-            codes = keep.tile([P, HALF], U32, name="x_codes%d" % hf, align_bytes=64)
-            scales = keep.tile([P, HALF], U8, name="x_scales%d" % hf, align_bytes=64)
-            nc.vector.quantize_mx(out=codes[:].bitcast(FP8X4), scales=scales[:], in_=x_grouped[:])
-            return codes, scales
+            return quantise("x%d" % half, x_grouped, HALF)
 
-        def same_field(hf, tag, align):
-            picked = keep.tile([P, TILES, HALF], F32, name="field%d" % hf, tag=tag, align_bytes=align)
+        def same_field(half, tag, align):
+            picked = keep.tile([P, TILES, HALF], F32, name="field", tag=tag, align_bytes=align)
             for t in range(TILES):
-                nc.vector.tensor_copy(picked[:, t, :], page[t][:].indirect(half_list(list4, hf)))
+                nc.vector.tensor_copy(picked[:, t, :], page[t][:].indirect(half_list(list4, half)))
             return picked
 
         reread(TILES - 1, 0)
         reread(TILES - 1, 1)
         x_quant = [quantise_x(0), quantise_x(1)]
-        field = [same_field(0, "after_scatter", None), same_field(1, "x_grouped0", 64)]
+        field = [same_field(0, "after_scatters", None), same_field(1, "x_grouped0", 64)]
 
-        spare = [key for key in raw]
+        free_tags = [raw_tag(*key) for key in raw]
 
-        def spare_tile(name, i):
-            w_name, t, a = spare[i]
-            return keep.tile([P, HALF], F32, name=name, tag="raw_%s_%d_%d" % (w_name, t, a))
+        def late_tile(name, i):
+            return keep.tile([P, HALF], F32, name=name, tag=free_tags[i])
 
-        def second_products(hf, t):
-            codes, scales = x_quant[hf]
+        def second_products(half, t):
+            codes, scales = x_quant[half]
             rows = slice(t * P, (t + 1) * P)
-            tag_p, bufs_p = (("bank_a", 2), ("bank_a", 2), ("bank_b", 1), ("bank_x", 2))[t]
-            tag_q, bufs_q = (("bank_c", 2), ("bank_c", 2), ("bank_h", 1), ("bank_x", 2))[t]
-            bank_p = psum.tile([P, HALF], F32, name="bank_p", tag=tag_p, bufs=bufs_p)
+            bank_p = new_bank(("bank_a", "bank_a", "bank_b", "bank_x")[t])
             nc.tensor.matmul_mx(
                 out=bank_p[:], lhsT=w4_codes[:, rows].bitcast(FP8X4), lhsT_scale=w4_sc[:, rows],
                 rhs=codes[:].bitcast(FP8X4), rhs_scale=scales[:], start=True, stop=True,
             )
-            bank_q = psum.tile([P, HALF], F32, name="bank_q", tag=tag_q, bufs=bufs_q)
+            bank_q = new_bank(("bank_c", "bank_c", "bank_h", "bank_x")[t])
             nc.tensor.matmul_mx(
                 out=bank_q[:], lhsT=w5_w[:, rows].bitcast(FP8X4), lhsT_scale=w5_sc[:, rows],
                 rhs=codes[:].bitcast(FP8X4), rhs_scale=scales[:], start=True, stop=True,
             )
-            if (hf, t) == (1, TILES - 1):
-                squashed = keep.tile([P, HALF], F32, name="squashed_last", tag="after_products")
-            else:
-                squashed = spare_tile("squashed", 3 * TILES + t)
+            squashed = late_tile("squashed", 3 * TILES + t)
             nc.scalar.activation(squashed[:], bank_p[:], ACT.Tanh)
-            y_sb = spare_tile("y_sb", hf * TILES + t)
+            y_sb = late_tile("y_sb", half * TILES + t)
             nc.vector.tensor_tensor(y_sb[:], bank_q[:], squashed[:], ALU.mult)
             return y_sb
 
-        def store(hf, t, result):
-            nc.sync.dma_start(out=out[t * P:(t + 1) * P, hf * HALF:(hf + 1) * HALF], in_=result)
-
-        scaled = keep.tile([P, TILES, HALF], F32, name="scaled", tag="x_turned1")
-        for t in range(TILES):
-            nc.scalar.activation(scaled[:, t, :], field[0][:, t, :], ACT.Copy, scale=gf_col[:, t:t + 1])
-        for t in range(TILES):
-            y_sb = second_products(0, t)
-            result = spare_tile("result", 2 * TILES + t)
-            nc.gpsimd.tensor_tensor(result[:], scaled[:, t, :], y_sb[:], ALU.add)
-            store(0, t, result[:])
-        y_late = [second_products(1, t) for t in range(TILES)]
-        results = keep.tile([P, TILES, HALF], F32, name="results", tag="after_products")
-        for t in range(TILES):
+        def finish(half, t, y_sb):
+            result = late_tile("result", 2 * TILES + t)
             nc.vector.scalar_tensor_tensor(
-                results[:, t, :], field[1][:, t, :], gf_col[:, t:t + 1], y_late[t][:], ALU.mult, ALU.add
+                result[:], field[half][:, t, :], gf_col[:, t:t + 1], y_sb[:], ALU.mult, ALU.add
             )
-            store(1, t, results[:, t, :])
+            nc.sync.dma_start(out=out[t * P:(t + 1) * P, half * HALF:(half + 1) * HALF], in_=result[:])
+
+        steps = [(half, t) for half in range(2) for t in range(TILES)]
+        y_next = second_products(*steps[0])
+        for i, (half, t) in enumerate(steps):
+            y_sb = y_next
+            if i + 1 < len(steps):
+                y_next = second_products(*steps[i + 1])
+            finish(half, t, y_sb)

@@ -81,11 +81,12 @@ def tile_list_lint_classing_step_kernel(
 
         tab_w = []
 
-        def load_table(a):
+        def load_table(a, pieces):
             tile = keep.tile([P, T], U32, name="tab_w", tag="tab_w%d" % a, align_bytes=64)
-            nc.sync.dma_start(
-                out=tile[:].bitcast(I32), in_=tab_words[a].rearrange("p n i -> p (n i)").bitcast(I32)
-            )
+            words = tab_words[a].rearrange("p n i -> p (n i)").bitcast(I32)
+            for first in range(0, T, T // pieces):
+                cols = slice(first, first + T // pieces)
+                nc.sync.dma_start(out=tile[:, cols].bitcast(I32), in_=words[:, cols])
             tab_w.append(tile)
 
         raw = {}
@@ -115,13 +116,13 @@ def tile_list_lint_classing_step_kernel(
             return tile
 
         list1 = load_list(offs, "list1")
-        load_table(0)
+        load_table(0, 2)
         w2_w = keep.tile([P, PASSES * 2 * H], U8, name="w2_w", align_bytes=64)
         nc.sync.dma_start(
             out=w2_w[:].bitcast(I32).rearrange("p (a n) -> p a n", a=PASSES),
             in_=w2_words.bitcast(I32).rearrange("a p n -> p a n"),
         )
-        load_table(1)
+        load_table(1, 1)
         load_weights(0)
         list2 = load_list(offs2, "list2")
         wgs0 = keep.tile([P, HALF], F32, name="wgs0")
@@ -129,17 +130,17 @@ def tile_list_lint_classing_step_kernel(
         load_page(0)
         load_weights(1)
         list3 = load_list(offs3, "list3")
-        load_weights(2)
         wgs1 = keep.tile([P, HALF], F32, name="wgs1", tag="after_scatters")
         nc.sync.dma_start(out=wgs1[:], in_=wgs[:, HALF:S])
         wgs_half = [wgs0, wgs1]
+        load_weights(2)
         sc_col = load_row_values(sc, "sc_col")
         load_page(1)
         load_weights(3)
         load_page(2)
-        load_page(3)
         raw_w4 = keep.tile([P, PACK, H], F32, name="raw_w4")
         nc.sync.dma_start(out=raw_w4[:], in_=w4.rearrange("(p i) c -> p i c", i=PACK))
+        load_page(3)
         w5_w = keep.tile([P, H], U32, name="w5_w", align_bytes=64)
         nc.sync.dma_start(
             out=w5_w[:].bitcast(I32), in_=w5_words[0].rearrange("p n i -> p (n i)").bitcast(I32)
@@ -186,7 +187,7 @@ def tile_list_lint_classing_step_kernel(
                 grouped = work.tile([P, PASSES * K_PASS], BF16, name="grouped", align_bytes=64, bufs=3)
                 for a in range(PASSES):
                     dst, src = interleave_views(grouped[:, a * K_PASS:(a + 1) * K_PASS], raw[(name, t, a)][:])
-                    if (name, t, a) == ("w3", 0, PASSES - 1):
+                    if (name, t) == ("w3", 0):
                         nc.vector.tensor_copy(dst, src)
                     else:
                         nc.scalar.activation(dst, src, ACT.Copy, scale=sign)
@@ -286,10 +287,10 @@ def tile_list_lint_classing_step_kernel(
             )
 
         quantise_weights(0)
-        b_first = [
-            copied_out(first_product(["w2"], c, ("bank_b", "bank_h")[c], c == 0), "b_sb", AHEAD + 1)
-            for c in range(2)
-        ]
+        b_both = keep.tile([P, 2, HALF], F32, name="b_both", tag=raw_tag("w1", 0, PASSES - 1))
+        b_first = [b_both[:, c, :] for c in range(2)]
+        for c in range(2):
+            nc.scalar.copy(b_first[c], first_product(["w2"], c, ("bank_b", "bank_h")[c], c == 0)[:])
         dist_first = [subtracted(first_product(["w1"], c, "bank_a", c == 0), b_first[c]) for c in range(2)]
         prod_first = [gate(dist_first[c], first_product(["w3"], c, "bank_c", c == 0)) for c in range(2)]
         h_first = work.tile([P, HALF], F32, name="h_first", bufs=1)

@@ -157,10 +157,10 @@ def tile_list_lint_classing_step_kernel(
         nc.vector.tensor_copy(v_sc[:], tab_sc[:].indirect(list1[:]))
         v_planes = []
         v_w = {}
-        for a, tag in enumerate(("v_plane0", "tab_w0")):
-            plane = zeroed_plane(tag, S, nc.vector)
+        for a, queue in enumerate((nc.scalar, nc.gpsimd)):
+            plane = zeroed_plane("v_plane%d" % a, S, nc.vector)
             for q in range(QUADS):
-                nc.scalar.dma_start(
+                queue.dma_start(
                     out=plane[32 * q:32 * q + 4, :].bitcast(I32),
                     in_=v_sc[16 * a + 4 * q:16 * a + 4 * q + 4, :].bitcast(I32),
                 )

from contextlib import ExitStack

import concourse.mybir as mybir
from concourse.masks import make_identity

K, H, T, S, T2, M = 1024, 512, 4096, 1024, 2048, 1024
FLOPS = 2 * (3 * K * H * S + 2 * H * H * M)

F32 = mybir.dt.float32
BF16 = mybir.dt.bfloat16
I32 = mybir.dt.int32
U32 = mybir.dt.uint32
U16 = mybir.dt.uint16
U8 = mybir.dt.uint8
FP8X4 = mybir.dt.float8_e4m3fn_x4
FP4X4 = mybir.dt.float4_e2m1fn_x4
ALU = mybir.AluOpType
ACT = mybir.ActivationFunctionType

P = 128
PACK = 4
K_PASS = P * PACK
PASSES = K // K_PASS
QUADS = 4
TILES = H // P
HALF = 512
BLOCKS = HALF // P
LIST_COLS = HALF // 16
CHUNKS = 2 * TILES
AHEAD = 3


def tile_list_lint_classing_step_kernel(
    tc, tab_words, tab_scales, offs, offs2, offs3, offs4, w1, w2_words, w2_scales, w3,
    wgs, page0, sc, w4, w5_words, w5_scales, gf, out,
):
    nc = tc.nc
    with ExitStack() as ctx:
        lists = ctx.enter_context(tc.tile_pool(name="lists", bufs=1))
        keep = ctx.enter_context(tc.tile_pool(name="keep", bufs=1))
        work = ctx.enter_context(tc.tile_pool(name="work", bufs=2))
        psum = ctx.enter_context(tc.psum_pool(name="psum", bufs=2))

        def load_list(src, name):
            tile = lists.tile([P, S // 16], U16, name=name)
            nc.sync.dma_start(tile[:], src)
            return tile

        def half_list(tile, half):
            return tile[:, half * LIST_COLS:(half + 1) * LIST_COLS]

        def zeroed_plane(tag, width, engine):
            plane = keep.tile([P, width], U8, name="plane", tag=tag, align_bytes=64)
            engine.memset(plane[:].bitcast(I32), 0)
            return plane

        tab_sc = keep.tile([P, T], U8, name="tab_sc", align_bytes=64)
        nc.sync.dma_start(
            out=tab_sc[0:32, :].bitcast(I32), in_=tab_scales.rearrange("a g n -> (a g) n").bitcast(I32)
        )
        nc.vector.memset(tab_sc[32:64, :].bitcast(I32), 0)
        nc.vector.memset(tab_sc[64:P, :].bitcast(I32), 0)

        w2_sc = zeroed_plane("w2_sc", PASSES * H, nc.gpsimd)
        for q in range(QUADS):
            nc.scalar.dma_start(
                out=w2_sc[32 * q:32 * q + 4, :].bitcast(I32).rearrange("g (a c) -> g a c", a=PASSES),
                in_=w2_scales[:, 4 * q:4 * q + 4, :].bitcast(I32).rearrange("a g c -> g a c"),
            )
        w5_sc = zeroed_plane("w5_sc", H, nc.vector)

        warm_in = keep.tile([P, 1], F32, name="warm_in")
        nc.vector.memset(warm_in[:], 0.0)
        warm_out = keep.tile([P, 1], F32, name="warm_out")
        nc.scalar.activation(warm_out[:], warm_in[:], ACT.Tanh)

        ident32 = keep.tile([P, P], F32, name="ident32")
        make_identity(nc, ident32[:])
        ident16 = keep.tile([P, P], BF16, name="ident16")
        make_identity(nc, ident16[:])

        tab_w = []

        def load_table(a, pieces):
            tile = keep.tile([P, T], U32, name="tab_w", tag="tab_w%d" % a, align_bytes=64)
            words = tab_words[a].rearrange("p n i -> p (n i)").bitcast(I32)
            for first in range(0, T, T // pieces):
                cols = slice(first, first + T // pieces)
                nc.sync.dma_start(out=tile[:, cols].bitcast(I32), in_=words[:, cols])
            tab_w.append(tile)

        raw = {}

        def raw_tag(name, t, a):
            return "raw_%s_%d_%d" % (name, t, a)

        def load_weights(t):
            for name, w in (("w1", w1), ("w3", w3)):
                for a in range(PASSES):
                    tile = keep.tile([P, PACK, P], F32, name="raw", tag=raw_tag(name, t, a))
                    rows = w[a * K_PASS:(a + 1) * K_PASS, t * P:(t + 1) * P]
                    nc.sync.dma_start(out=tile[:], in_=rows.rearrange("(p i) c -> p i c", i=PACK))
                    raw[(name, t, a)] = tile

        page = []

        def load_page(t):
            tile = keep.tile([P, T2], F32, name="page%d" % t)
            nc.sync.dma_start(out=tile[:], in_=page0[t * P:(t + 1) * P, :])
            page.append(tile)

        def load_row_values(src, name):
            tile = keep.tile([P, TILES], F32, name=name)
            with nc.allow_non_contiguous_dma(reason="one value for each row of a tile"):
                nc.sync.dma_start(out=tile[:], in_=src.rearrange("(t p) -> p t", p=P))
            return tile

        list1 = load_list(offs, "list1")
        load_table(0, 2)
        w2_w = keep.tile([P, PASSES * 2 * H], U8, name="w2_w", align_bytes=64)
        nc.sync.dma_start(
            out=w2_w[:].bitcast(I32).rearrange("p (a n) -> p a n", a=PASSES),
            in_=w2_words.bitcast(I32).rearrange("a p n -> p a n"),
        )
        load_table(1, 1)
        load_weights(0)
        list2 = load_list(offs2, "list2")
        wgs0 = keep.tile([P, HALF], F32, name="wgs0")
        nc.sync.dma_start(out=wgs0[:], in_=wgs[:, 0:HALF])
        load_page(0)
        load_weights(1)
        list3 = load_list(offs3, "list3")
        wgs1 = keep.tile([P, HALF], F32, name="wgs1", tag="after_scatters")
        nc.sync.dma_start(out=wgs1[:], in_=wgs[:, HALF:S])
        wgs_half = [wgs0, wgs1]
        load_weights(2)
        sc_col = load_row_values(sc, "sc_col")
        load_page(1)
        load_weights(3)
        load_page(2)
        raw_w4 = keep.tile([P, PACK, H], F32, name="raw_w4")
        nc.sync.dma_start(out=raw_w4[:], in_=w4.rearrange("(p i) c -> p i c", i=PACK))
        load_page(3)
        w5_w = keep.tile([P, H], U32, name="w5_w", align_bytes=64)
        nc.sync.dma_start(
            out=w5_w[:].bitcast(I32), in_=w5_words[0].rearrange("p n i -> p (n i)").bitcast(I32)
        )
        for q in range(QUADS):
            nc.sync.dma_start(
                out=w5_sc[32 * q:32 * q + 4, :].bitcast(I32),
                in_=w5_scales[0, 4 * q:4 * q + 4, :].bitcast(I32),
            )
        list4 = load_list(offs4, "list4")
        gf_col = load_row_values(gf, "gf_col")

        v_sc = keep.tile([P, S], U8, name="v_sc", align_bytes=64)
        nc.vector.tensor_copy(v_sc[:], tab_sc[:].indirect(list1[:]))
        v_planes = []
        v_w = {}
        for a, queue in enumerate((nc.scalar, nc.gpsimd)):
            plane = zeroed_plane("v_plane%d" % a, S, nc.vector)
            for q in range(QUADS):
                queue.dma_start(
                    out=plane[32 * q:32 * q + 4, :].bitcast(I32),
                    in_=v_sc[16 * a + 4 * q:16 * a + 4 * q + 4, :].bitcast(I32),
                )
            v_planes.append(plane)
            for half in range(2):
                tile = keep.tile([P, HALF], U32, name="v_w%d_%d" % (a, half), align_bytes=64)
                nc.vector.tensor_copy(tile[:], tab_w[a][:].indirect(half_list(list1, half)))
                v_w[(a, half)] = tile

        def interleave_views(dst, src):
            return (dst.rearrange("p (c n i) -> p c i n", n=4, i=PACK),
                    src.rearrange("p i (c n) -> p c i n", n=4))

        def quantise(name, grouped, width):
            codes = keep.tile([P, width], U32, name="codes_" + name, align_bytes=64)
            scales = keep.tile([P, width], U8, name="scales_" + name, align_bytes=64)
            nc.vector.quantize_mx(out=codes[:].bitcast(FP8X4), scales=scales[:], in_=grouped[:])
            return codes, scales

        quant = {}

        def quantise_weights(t):
            for name, sign in (("w1", -1.0), ("w3", 1.0)):
                grouped = work.tile([P, PASSES * K_PASS], BF16, name="grouped", align_bytes=64, bufs=3)
                for a in range(PASSES):
                    dst, src = interleave_views(grouped[:, a * K_PASS:(a + 1) * K_PASS], raw[(name, t, a)][:])
                    if (name, t) == ("w3", 0):
                        nc.vector.tensor_copy(dst, src)
                    else:
                        nc.scalar.activation(dst, src, ACT.Copy, scale=sign)
                quant[(name, t)] = quantise("%s_%d" % (name, t), grouped, PASSES * P)

        def weight_operand(name, t, a):
            if name == "w2":
                first = a * H + t * P
                return w2_w[:, 2 * first:2 * (first + P)].bitcast(FP4X4), w2_sc[:, first:first + P]
            codes, scales = quant[(name, t)]
            return codes[:, a * P:(a + 1) * P].bitcast(FP8X4), scales[:, a * P:(a + 1) * P]

        bank_bufs = {"bank_a": 2, "bank_b": 1, "bank_c": 2, "bank_h": 1, "bank_x": 2}

        def new_bank(tag, dtype=F32):
            return psum.tile([P, HALF], dtype, name=tag, tag=tag, bufs=bank_bufs[tag])

        def first_product(names, c, tag, by_rows):
            t, half = divmod(c, 2)
            bank = new_bank(tag)
            terms = [(name, a) for name in names for a in range(PASSES)]
            width = HALF if by_rows else P
            for j0 in range(0, HALF, width):
                for i, (name, a) in enumerate(terms):
                    w_codes, w_plane = weight_operand(name, t, a)
                    v_codes = v_w[(a, half)][:, j0:j0 + width].bitcast(FP8X4)
                    first = half * HALF + j0
                    v_plane = v_planes[a][:, first:first + width]
                    flags = dict(start=(i == 0), stop=(i == len(terms) - 1))
                    if by_rows:
                        nc.tensor.matmul_mx(out=bank[:], lhsT=w_codes, lhsT_scale=w_plane,
                                            rhs=v_codes, rhs_scale=v_plane, **flags)
                    else:
                        nc.tensor.matmul_mx(out=bank[:, j0:j0 + P], lhsT=v_codes, lhsT_scale=v_plane,
                                            rhs=w_codes, rhs_scale=w_plane, **flags)
            return bank

        def copied_out(bank, name, bufs):
            tile = work.tile([P, HALF], F32, name=name, bufs=bufs)
            nc.scalar.copy(tile[:], bank[:])
            return tile

        def magnitude(src):
            dist = work.tile([P, HALF], F32, name="dist", bufs=AHEAD)
            nc.scalar.activation(dist[:], src[:], ACT.Abs)
            return dist

        def subtracted(bank_a, b_sb):
            diff = work.tile([P, HALF], F32, name="diff")
            nc.vector.tensor_tensor(diff[:], bank_a[:], b_sb[:], ALU.add)
            return magnitude(diff)

        def difference(c):
            bank_b = first_product(["w2"], c, "bank_b", False)
            if c % 2 == 0:
                dist = magnitude(first_product(["w2", "w1"], c, "bank_a", False))
                return dist, copied_out(bank_b, "b_sb", AHEAD + 1)
            bank_a = first_product(["w1"], c, "bank_a", False)
            b_sb = copied_out(bank_b, "b_sb", AHEAD + 1)
            return subtracted(bank_a, b_sb), b_sb

        def gate(dist, bank_c):
            prod = work.tile([P, HALF], F32, name="prod", bufs=4)
            nc.vector.tensor_tensor(prod[:], bank_c[:], dist[:], ALU.mult)
            return prod

        def new_tags(prod, b_sb):
            bank = new_bank("bank_h")
            for b in range(BLOCKS):
                cols = slice(b * P, (b + 1) * P)
                nc.tensor.matmul(bank[:, cols], lhsT=b_sb[:, cols], rhs=ident32[:],
                                 start=True, stop=False, is_transpose=True)
                nc.tensor.matmul(bank[:, cols], lhsT=prod[:, cols], rhs=ident32[:],
                                 start=False, stop=True, is_transpose=True)
            return copied_out(bank, "h_sb", 4)

        def scatter(c, h_sb):
            t, half = divmod(c, 2)
            nc.vector.tensor_tensor(
                page[t][:].indirect(half_list(list2, half)), h_sb[:], wgs_half[half][:], ALU.mult
            )

        x_turned = [keep.tile([P, BLOCKS, 2, P], F32, name="x_turned%d" % half) for half in range(2)]

        def reread(t, half):
            picked = work.tile([P, HALF], F32, name="picked")
            nc.vector.tensor_copy(picked[:], page[t][:].indirect(half_list(list3, half)))
            x_rows = work.tile([P, HALF], BF16, name="x_rows")
            nc.scalar.activation(x_rows[:], picked[:], ACT.Copy, scale=sc_col[:, t:t + 1])
            bank_x = new_bank("bank_x", BF16)
            for b in range(BLOCKS):
                cols = slice(b * P, (b + 1) * P)
                nc.tensor.transpose(bank_x[:, cols], x_rows[:, cols], ident16[:])
            nc.scalar.copy(
                x_turned[half][:, :, :, 32 * t:32 * (t + 1)],
                bank_x[:].bitcast(F32).rearrange("m (b q u) -> m b u q", b=BLOCKS, u=2),
            )

        quantise_weights(0)
        b_both = keep.tile([P, 2, HALF], F32, name="b_both", tag=raw_tag("w1", 0, PASSES - 1))
        b_first = [b_both[:, c, :] for c in range(2)]
        for c in range(2):
            nc.scalar.copy(b_first[c], first_product(["w2"], c, ("bank_b", "bank_h")[c], c == 0)[:])
        dist_first = [subtracted(first_product(["w1"], c, "bank_a", c == 0), b_first[c]) for c in range(2)]
        prod_first = [gate(dist_first[c], first_product(["w3"], c, "bank_c", c == 0)) for c in range(2)]
        h_first = work.tile([P, HALF], F32, name="h_first", bufs=1)
        nc.vector.tensor_tensor(h_first[:], prod_first[0][:], b_first[0][:], ALU.add)
        h_ready = {1: new_tags(prod_first[1], b_first[1])}
        scatter(0, h_first)
        quantise_weights(1)
        fronts = {2: difference(2)}
        banks_c = {2: first_product(["w3"], 2, "bank_c", False)}
        fronts[3] = difference(3)

        for c in range(1, CHUNKS):
            t, half = divmod(c, 2)
            if half == 1 and t + 2 < TILES:
                quantise_weights(t + 2)
            if c + 1 < CHUNKS:
                dist, b_sb = fronts[c + 1]
                prod = gate(dist, banks_c[c + 1])
                if c + 2 < CHUNKS:
                    banks_c[c + 2] = first_product(["w3"], c + 2, "bank_c", False)
                h_ready[c + 1] = new_tags(prod, b_sb)
            if c + AHEAD < CHUNKS:
                fronts[c + AHEAD] = difference(c + AHEAD)
            if t > 0:
                reread(t - 1, half)
            scatter(c, h_ready[c])
            if c == CHUNKS - 2:
                grouped4 = keep.tile([P, PACK * H], BF16, name="grouped4", align_bytes=64)
                dst, src = interleave_views(grouped4[:], raw_w4[:])
                nc.scalar.activation(dst, src, ACT.Copy)
                w4_codes, w4_sc = quantise("w4", grouped4, H)

        def quantise_x(half):
            x_grouped = keep.tile([P, PACK * HALF], BF16, name="x_grouped", tag="x_grouped%d" % half,
                                  align_bytes=64)
            words = x_grouped[:].bitcast(F32)
            for pair in range(BLOCKS // 2):
                bank_x = new_bank("bank_x")
                for b in range(2):
                    for u in range(2):
                        cols = slice((2 * b + u) * P, (2 * b + u + 1) * P)
                        nc.tensor.transpose(bank_x[:, cols], x_turned[half][:, 2 * pair + b, u, :], ident32[:])
                nc.scalar.copy(
                    words[:, pair * HALF:(pair + 1) * HALF].rearrange("p (b m u) -> p b m u", b=2, u=2),
                    bank_x[:].rearrange("p (b u m) -> p b m u", b=2, u=2),
                )
            return quantise("x%d" % half, x_grouped, HALF)

        def same_field(half, tag, align):
            picked = keep.tile([P, TILES, HALF], F32, name="field", tag=tag, align_bytes=align)
            for t in range(TILES):
                nc.vector.tensor_copy(picked[:, t, :], page[t][:].indirect(half_list(list4, half)))
            return picked

        reread(TILES - 1, 0)
        reread(TILES - 1, 1)
        x_quant = [quantise_x(0), quantise_x(1)]
        field = [same_field(0, "after_scatters", None), same_field(1, "x_grouped0", 64)]

        free_tags = [raw_tag(*key) for key in raw]

        def late_tile(name, i):
            return keep.tile([P, HALF], F32, name=name, tag=free_tags[i])

        def second_products(half, t):
            codes, scales = x_quant[half]
            rows = slice(t * P, (t + 1) * P)
            bank_p = new_bank(("bank_a", "bank_a", "bank_b", "bank_x")[t])
            nc.tensor.matmul_mx(
                out=bank_p[:], lhsT=w4_codes[:, rows].bitcast(FP8X4), lhsT_scale=w4_sc[:, rows],
                rhs=codes[:].bitcast(FP8X4), rhs_scale=scales[:], start=True, stop=True,
            )
            bank_q = new_bank(("bank_c", "bank_c", "bank_h", "bank_x")[t])
            nc.tensor.matmul_mx(
                out=bank_q[:], lhsT=w5_w[:, rows].bitcast(FP8X4), lhsT_scale=w5_sc[:, rows],
                rhs=codes[:].bitcast(FP8X4), rhs_scale=scales[:], start=True, stop=True,
            )
            squashed = late_tile("squashed", 3 * TILES + t)
            nc.scalar.activation(squashed[:], bank_p[:], ACT.Tanh)
            y_sb = late_tile("y_sb", half * TILES + t)
            nc.vector.tensor_tensor(y_sb[:], bank_q[:], squashed[:], ALU.mult)
            return y_sb

        def finish(half, t, y_sb):
            result = late_tile("result", 2 * TILES + t)
            nc.vector.scalar_tensor_tensor(
                result[:], field[half][:, t, :], gf_col[:, t:t + 1], y_sb[:], ALU.mult, ALU.add
            )
            nc.sync.dma_start(out=out[t * P:(t + 1) * P, half * HALF:(half + 1) * HALF], in_=result[:])

        steps = [(half, t) for half in range(2) for t in range(TILES)]
        y_next = second_products(*steps[0])
        for i, (half, t) in enumerate(steps):
            y_sb = y_next
            if i + 1 < len(steps):
                y_next = second_products(*steps[i + 1])
            finish(half, t, y_sb)
